import numpy as np
import ml_dtypes


def mxq(x, axis, fmt="e4m3"):
    dtype, down = {"e4m3": (ml_dtypes.float8_e4m3fn, 7), "e5m2": (ml_dtypes.float8_e5m2, 14)}[fmt]
    v = np.moveaxis(np.asarray(x, np.float32).astype(ml_dtypes.bfloat16).astype(np.float64), axis, -1)
    blocks = v.reshape(v.shape[:-1] + (-1, 32))
    amax = np.abs(blocks).max(-1, keepdims=True)
    byte = np.maximum(np.where(amax > 0, np.frexp(amax)[1] - 1 + 127, 0) - down, 1)
    scale = np.exp2(byte - 127.0)
    codes = (blocks / scale).astype(np.float32).astype(dtype).astype(np.float64)
    return np.moveaxis((codes * scale).reshape(v.shape), -1, axis)


WIDE = False


def mx_kscale(k):
    if not WIDE:
        return np.ones(k)
    levels = np.array([24, -24, 12, -12, 0])
    if k % 512:
        return np.exp2(np.random.permutation(np.resize(levels, k // 32))).repeat(32)
    a = np.empty((k // 512, 16))
    for p in range(k // 512):
        a[p, :8] = np.random.permutation(np.resize(levels, 8))
        for g in range(8):
            far = levels[np.abs(levels - a[p, g]) >= 10]
            a[p, g + 8] = far[np.random.randint(len(far))]
    return np.exp2(a.ravel()).repeat(32)


def f64(x):
    return np.asarray(x).astype(np.float64)


def striped8(idx):
    return np.concatenate([v.reshape(-1, 16).T for v in idx]).astype(np.uint16)


def unstriped8(offs):
    return np.stack([offs[16 * g:16 * g + 16].T.reshape(-1) for g in range(8)]).astype(np.int64)


E2M1 = np.array([0.0, 0.5, 1.0, 1.5, 2.0, 3.0, 4.0, 6.0, -0.0, -0.5, -1.0, -1.5, -2.0, -3.0, -4.0, -6.0])


def pack_weight(w, fmt):
    k, n = w.shape
    w = f64(np.asarray(w, np.float32).astype(ml_dtypes.bfloat16)).reshape(k // 32, 32, n)
    amax = np.abs(w).max(1)
    if fmt == "e4m3":
        byte = np.frexp(amax)[1] - 1 + 127 - 7
    else:
        mant, ex = np.frexp(amax / 6.0)
        byte = np.where(mant > 0.5, ex, ex - 1) + 127
    byte = np.clip(np.where(amax > 0, byte, 1), 1, 254)
    scaled = (w * np.exp2(127.0 - byte)[:, None, :]).reshape(k, n).astype(np.float32)
    by_word = np.ascontiguousarray(scaled.reshape(k // 512, 128, 4, n).transpose(0, 1, 3, 2))
    if fmt == "e4m3":
        words = by_word.astype(ml_dtypes.float8_e4m3fn).view(np.uint8)
    else:
        c = by_word.astype(ml_dtypes.float4_e2m1fn).view(np.uint8) & 0xF
        words = (c[..., 0::2] | (c[..., 1::2] << 4)).reshape(k // 512, 128, 2 * n)
    return np.ascontiguousarray(words), np.ascontiguousarray(byte.astype(np.uint8).reshape(k // 512, 16, n))


def unpack_weight(words, scales, fmt):
    g, _, n = scales.shape
    words = np.ascontiguousarray(words).reshape(g, 128, n, -1)
    if fmt == "e4m3":
        vals = words.view(ml_dtypes.float8_e4m3fn).astype(np.float64)
    else:
        nib = np.empty((g, 128, n, 4), np.uint8)
        nib[..., 0::2] = words & 0xF
        nib[..., 1::2] = words >> 4
        vals = E2M1[nib]
    vals = vals * np.repeat(np.exp2(scales.astype(np.float64) - 127.0), 8, axis=1)[..., None]
    return vals.transpose(0, 1, 3, 2).reshape(g * 512, n)


def planes(y):
    n, m = y.shape
    v = y.astype(np.float32).astype(ml_dtypes.bfloat16).astype(np.float64).reshape(n // 32, 32, m)
    top = np.abs(v).max(1)
    byte = np.clip(np.where(top > 0, np.frexp(top)[1] - 1 + 127 - 7, 1), 1, 254)
    codes = (v * np.exp2(127.0 - byte)[:, None, :]).reshape(n, m).astype(np.float32).astype(ml_dtypes.float8_e4m3fn).view(np.uint8)
    words = codes.reshape(n // 512, 128, 4, m).transpose(0, 1, 3, 2)
    return np.ascontiguousarray(words), np.ascontiguousarray(byte.astype(np.uint8).reshape(n // 512, 16, m))


K, N, T, J = 512, 512, 2048, 512


def setup_inputs():
    n = np.random.standard_normal
    s = mx_kscale(K)[:, None]
    p_w4 = pack_weight(n((K, N)) / np.sqrt(K) / s, "e2m1")
    return {
        "xT": (n((K, T)) * s).astype(np.float32),
        "wgt": np.repeat(np.random.uniform(0.5, 2.0, (8, 3 * J)), 16, axis=0).astype(np.float32),
        "w4_words": p_w4[0],
        "w4_scales": p_w4[1],
        "wd": (0.4 * (n((K, N)) / np.sqrt(K) / s)).astype(np.float32),
        "b": (0.3 * n(N)).astype(np.float32),
        "offs": striped8(np.stack([np.concatenate([np.random.permutation(T)[:J] for _ in range(3)]) for _ in range(8)])),
    }


def reference(xT, wgt, w4_words, w4_scales, wd, b, offs):
    idx = unstriped8(offs)
    rows = np.arange(K)
    xg = f64(wgt)[rows // 4 % 128] * f64(xT)[rows[:, None], idx[rows % 512 // 64]]
    xT_ = mxq(xg, 0, "e4m3").reshape(K, 3, J)
    w4_ = unpack_weight(w4_words, w4_scales, "e2m1")
    wd_ = mxq(f64(wd), 0, "e4m3")
    a0 = w4_.T @ xT_[:, 0] + wd_.T @ xT_[:, 0]
    a1 = w4_.T @ xT_[:, 1] + wd_.T @ xT_[:, 1]
    a2 = w4_.T @ xT_[:, 2] + wd_.T @ xT_[:, 2]
    out_0 = np.maximum(a0, 0.0) + np.maximum(a1, 0.0) + np.maximum(a2, 0.0) + f64(b)[:, None]
    return (out_0,) + planes(out_0)

@@ -1,0 +1,290 @@
+from contextlib import ExitStack
+
+import concourse.mybir as mybir
+
+K, N, T, J = 512, 512, 2048, 512
+PICKS = 3
+P = 128
+PACK = 4
+FLOPS = 2 * 2 * K * N * J * PICKS
+
+F32 = mybir.dt.float32
+BF16 = mybir.dt.bfloat16
+I32 = mybir.dt.int32
+U32 = mybir.dt.uint32
+U16 = mybir.dt.uint16
+U8 = mybir.dt.uint8
+FP8X4 = mybir.dt.float8_e4m3fn_x4
+FP4X4 = mybir.dt.float4_e2m1fn_x4
+ALU = mybir.AluOpType
+ACT = mybir.ActivationFunctionType
+
+UNITS = [(0, 0, 256), (1, 0, 256), (2, 0, 256), (0, 256, 256), (1, 256, 256), (2, 256, 128), (2, 384, 128)]
+VECTOR_SLICES = ((3,2),)
+
+
+def tile_list_dl_relus_biasP_kernel(
+    tc, xT, wgt, w4_words, w4_scales, wd, b, offs, out_0, out_1, out_2
+):
+    nc = tc.nc
+    with ExitStack() as ctx:
+        sb = ctx.enter_context(tc.tile_pool(name="sb", bufs=1))
+        ps = ctx.enter_context(tc.psum_pool(name="ps", bufs=1))
+
+        def tile(shape, dtype, name):
+            return sb.tile(shape, dtype, name=name, align_bytes=64)
+
+        lists = sb.tile([P, PICKS * J // 16], U16, name="lists")
+        x = [tile([P, T], F32, "x%d" % i) for i in range(PACK)]
+        wg = [tile([P, J], F32, "wg%d" % c) for c in range(PICKS)]
+        w4_raw = tile([P, 2 * N], U8, "w4_raw")
+        s4_raw = tile([P, N], U8, "s4_raw")
+        wd_raw = tile([P, PACK, N], F32, "wd_raw")
+        bias = tile([P, PACK], F32, "bias")
+        x_rows = xT.rearrange("(p i) t -> p i t", i=PACK)
+        nc.sync.dma_start(lists[:], offs)
+        nc.gpsimd.memset(s4_raw[:].bitcast(I32), 0)
+        for q in range(4):
+            nc.scalar.dma_start(
+                out=s4_raw[32 * q : 32 * q + 4, :].bitcast(I32),
+                in_=w4_scales[0, 4 * q : 4 * q + 4, :].bitcast(I32),
+            )
+        nc.sync.dma_start(out=x[0][:], in_=x_rows[:, 0, :])
+        nc.sync.dma_start(out=wg[0][:], in_=wgt[:, 0:J])
+        nc.sync.dma_start(out=wg[1][:], in_=wgt[:, J : 2 * J])
+        nc.sync.dma_start(out=x[1][:], in_=x_rows[:, 1, :])
+        nc.sync.dma_start(out=w4_raw[:].bitcast(I32), in_=w4_words[0].bitcast(I32))
+        nc.sync.dma_start(out=wg[2][:], in_=wgt[:, 2 * J : 3 * J])
+        nc.scalar.dma_start(out=bias[:], in_=b.rearrange("(p t) -> p t", t=PACK))
+        nc.sync.dma_start(out=x[2][:], in_=x_rows[:, 2, :])
+        nc.sync.dma_start(out=wd_raw[:], in_=wd.rearrange("(p i) n -> p i n", i=PACK))
+        nc.sync.dma_start(out=x[3][:], in_=x_rows[:, 3, :])
+
+        w4 = tile([P, 2 * N], U8, "w4")
+        s4 = tile([P, N], U8, "s4")
+        units = UNITS
+        low = [tile([P, 2, J], F32, "low%d" % c) for c in range(PICKS)]
+        xq = [tile([P, w], U32, "xq%d" % u) for u, (c, j0, w) in enumerate(units)]
+        xs = [tile([P, w], U8, "xs%d" % u) for u, (c, j0, w) in enumerate(units)]
+        wd_b = tile([P, N, PACK], BF16, "wd_b")
+        wd_q = tile([P, N], U32, "wd_q")
+        wd_s = tile([P, N], U8, "wd_s")
+        xb = {}
+        high = {}
+        totals = {}
+        banks = {}
+        y_b = {}
+        y_rows = out_0.rearrange("(p t) j -> p t j", t=PACK)
+        y_words = out_1[0].rearrange("p j i -> p (j i)").bitcast(I32)
+        y_s = tile([P, J], U8, "y_s")
+        SUB = {4: 0}
+        AFTER = {2: "xb1"}
+        for u, (c, j0, w) in enumerate(units):
+            if u in SUB:
+                both = tile([P, 3 * 256], F32, "both%d" % u)
+                high[u] = both[:, 0 : 2 * w].rearrange("p (i j) -> p i j", i=2)
+                xb[SUB[u]] = both[:, 256:768].bitcast(BF16).rearrange("p (j i) -> p j i", i=PACK)
+        last = tile([P, PACK * 256], F32, "last")
+        xb[3] = last[:, 512:1024].bitcast(BF16).rearrange("p (j i) -> p j i", i=PACK)
+        last4 = last[:].rearrange("p (i j) -> p i j", i=PACK)
+        for u, (c, j0, w) in enumerate(units):
+            if u not in xb:
+                xb[u] = tile([P, w, PACK], BF16, "xb%d" % u)[:]
+
+        def s4copy():
+            nc.vector.tensor_copy(
+                out=s4[:].rearrange("p (t q) -> p t q", t=PACK),
+                in_=s4_raw[:].rearrange("p (q t) -> p t q", t=PACK),
+            )
+
+        def w4copy():
+            nc.scalar.copy(
+                out=w4[:].bitcast(U16).rearrange("p (t q) -> p t q", t=PACK),
+                in_=w4_raw[:].bitcast(U16).rearrange("p (q t) -> p t q", t=PACK),
+            )
+
+        def gather(dst, i, c, j0, w):
+            first = (c * J + j0) // 16
+            nc.vector.tensor_tensor(
+                dst, x[i][:].indirect(lists[:, first : first + w // 16]), wg[c][:, j0 : j0 + w], ALU.mult
+            )
+
+        def gl(i, c):
+            gather(low[c][:, i, :], i, c, 0, J)
+
+        def ga(i):
+            gather(low[2][:, i, 0:256], i, 2, 0, 256)
+
+        def g4(i, j0, w):
+            gather(last4[:, i, j0 - 256 : j0 - 256 + w], i, 2, j0, w)
+
+        def weave4(u):
+            c, j0, w = units[u]
+            nc.scalar.activation(
+                out=xb[u].rearrange("p (g e) i -> p g i e", e=4),
+                in_=last4[:, :, j0 - 256 : j0 - 256 + w].rearrange("p i (g e) -> p g i e", e=4), func=ACT.Copy
+            )
+
+        def gh(i, u):
+            c, j0, w = units[u]
+            if u not in high:
+                high[u] = tile([P, 2, w], F32, AFTER.get(u, "high%d" % u))[:]
+            gather(high[u][:, i - 2, :], i, c, j0, w)
+
+        def weave(u, half):
+            c, j0, w = units[u]
+            src = low[c][:, :, j0 : j0 + w] if half == 0 else high[u]
+            nc.scalar.activation(
+                out=xb[u][:, :, 2 * half : 2 * half + 2], in_=src.rearrange("p i j -> p j i"), func=ACT.Copy
+            )
+
+        def quantise(codes, scales, src):
+            nc.vector.quantize_mx(out=codes.bitcast(FP8X4), scales=scales, in_=src.rearrange("p j i -> p (j i)"))
+
+        def q(u):
+            quantise(xq[u][:], xs[u][:], xb[u])
+
+        def wdweave():
+            nc.scalar.activation(
+                out=wd_b[:].rearrange("p (t q) i -> p q i t", t=PACK),
+                in_=wd_raw[:].rearrange("p i (q t) -> p q i t", t=PACK),
+                func=ACT.Copy,
+            )
+
+        def qwd():
+            quantise(wd_q[:], wd_s[:], wd_b[:])
+
+        def mm(u):
+            c, j0, w = units[u]
+            per_bank = J // w
+            totals[u] = tile([P, PACK, w], F32, "total%d" % u)
+            for t0 in range(0, PACK, per_bank):
+                bank = ps.tile([P, per_bank, w], F32, name="acc", tag="bank%d" % (len(banks) % 8))
+                banks[u, t0] = bank
+                for t in range(t0, t0 + per_bank):
+                    cols = slice(t * P, (t + 1) * P)
+                    nc.tensor.matmul_mx(
+                        bank[:, t - t0, :], lhsT=w4[:, 2 * t * P : 2 * (t + 1) * P].bitcast(FP4X4), lhsT_scale=s4[:, cols],
+                        rhs=xq[u][:].bitcast(FP8X4), rhs_scale=xs[u][:], start=True, stop=False,
+                    )
+                    nc.tensor.matmul_mx(
+                        bank[:, t - t0, :], lhsT=wd_q[:, cols].bitcast(FP8X4), lhsT_scale=wd_s[:, cols],
+                        rhs=xq[u][:].bitcast(FP8X4), rhs_scale=xs[u][:], start=False, stop=True,
+                    )
+
+        def epi(u, before=None):
+            c, j0, w = units[u]
+            per_bank = J // w
+            total = totals[u]
+            for t0 in range(0, PACK, per_bank):
+                bank = banks[u, t0]
+                if c > 0:
+                    off = j0 - units[before][1]
+                    nc.vector.scalar_tensor_tensor(
+                        total[:, t0 : t0 + per_bank, :], bank[:], 0.0,
+                        totals[before][:, t0 : t0 + per_bank, off : off + w], ALU.max, ALU.add
+                    )
+                elif (u, t0) in VECTOR_SLICES:
+                    for t in range(t0, t0 + per_bank):
+                        nc.vector.tensor_scalar(
+                            total[:, t, :], bank[:, t - t0, :], 0.0, bias[:, t : t + 1], ALU.max, ALU.add
+                        )
+                else:
+                    nc.scalar.activation(out=total[:, t0 : t0 + per_bank, :], in_=bank[:], func=ACT.Relu)
+                    for t in range(t0, t0 + per_bank):
+                        nc.scalar.activation(
+                            out=total[:, t, :], in_=total[:, t, :], func=ACT.Identity, bias=bias[:, t : t + 1]
+                        )
+
+        def store(u):
+            c, j0, w = units[u]
+            nc.sync.dma_start(out=y_rows[:, :, j0 : j0 + w], in_=totals[u][:])
+
+        def ybf(u, eng):
+            c, j0, w = units[u]
+            y_b[u] = tile([P, w, PACK], BF16, "y_b%d" % u)
+            woven = y_b[u][:].rearrange("p (g e) t -> p g t e", e=4)
+            source = totals[u][:].rearrange("p t (g e) -> p g t e", e=4)
+            if eng == "S":
+                nc.scalar.activation(out=woven, in_=source, func=ACT.Copy)
+            else:
+                nc.vector.tensor_copy(out=woven, in_=source)
+
+        def yq(u):
+            c, j0, w = units[u]
+            y_q = tile([P, w], U32, "y_q%d" % u)
+            quantise(y_q[:], y_s[:, j0 : j0 + w], y_b[u][:])
+            nc.sync.dma_start(out=y_words[:, j0 : j0 + w], in_=y_q[:].bitcast(I32))
+
+        gl(0,0)
+        gl(0,1)
+        s4copy()
+        w4copy()
+        gl(1,0)
+        weave(0,0)
+        weave(3,0)
+        gl(1,1)
+        weave(1,0)
+        weave(4,0)
+        ga(0)
+        ga(1)
+        weave(2,0)
+        g4(0,256,256)
+        g4(1,256,256)
+        wdweave()
+        gh(2,0)
+        gh(2,1)
+        gh(2,3)
+        gh(2,4)
+        gh(3,0)
+        weave(0,1)
+        gh(3,1)
+        weave(1,1)
+        qwd()
+        gh(3,3)
+        weave(3,1)
+        q(0)
+        mm(0)
+        gh(3,4)
+        weave(4,1)
+        q(1)
+        mm(1)
+        epi(0)
+        gh(2,2)
+        gh(3,2)
+        weave(2,1)
+        q(3)
+        mm(3)
+        g4(2,256,256)
+        g4(3,256,128)
+        weave4(5)
+        q(4)
+        mm(4)
+        g4(3,384,128)
+        weave4(6)
+        q(2)
+        mm(2)
+        epi(1,0)
+        q(5)
+        q(6)
+        epi(2,1)
+        store(2)
+        mm(5)
+        epi(3)
+        mm(6)
+        ybf(2,"S")
+        epi(4,3)
+        yq(2)
+        epi(5,4)
+        store(5)
+        ybf(5,"S")
+        epi(6,4)
+        store(6)
+        yq(5)
+        ybf(6,"V")
+        yq(6)
+        for k in range(4):
+            queue = nc.scalar if k % 2 else nc.sync
+            queue.dma_start(
+                out=out_2[0, 4 * k : 4 * k + 4, :].bitcast(I32), in_=y_s[32 * k : 32 * k + 4, :].bitcast(I32)
+            )

@@ -20,7 +20,7 @@ ALU = mybir.AluOpType
 ACT = mybir.ActivationFunctionType
 
 UNITS = [(0, 0, 256), (1, 0, 256), (2, 0, 256), (0, 256, 256), (1, 256, 256), (2, 256, 128), (2, 384, 128)]
-VECTOR_SLICES = ((3,2),)
+VECTOR_SLICES = ((0, 2), (3, 0))
 
 
 def tile_list_dl_relus_biasP_kernel(
@@ -43,19 +43,22 @@ def tile_list_dl_relus_biasP_kernel(
         bias = tile([P, PACK], F32, "bias")
         x_rows = xT.rearrange("(p i) t -> p i t", i=PACK)
         nc.sync.dma_start(lists[:], offs)
-        nc.gpsimd.memset(s4_raw[:].bitcast(I32), 0)
+        s4_rows = tile([P, N // 4], I32, "s4_rows")
         for q in range(4):
             nc.scalar.dma_start(
-                out=s4_raw[32 * q : 32 * q + 4, :].bitcast(I32),
-                in_=w4_scales[0, 4 * q : 4 * q + 4, :].bitcast(I32),
+                out=s4_rows[32 * q : 32 * q + 4, :], in_=w4_scales[0, 4 * q : 4 * q + 4, :].bitcast(I32)
             )
+        nc.vector.memset(s4_raw[:].bitcast(I32), 0)
+        for q in range(4):
+            nc.vector.tensor_copy(out=s4_raw[32 * q : 32 * q + 4, :].bitcast(I32), in_=s4_rows[32 * q : 32 * q + 4, :])
+        nc.sync.dma_start(out=wg[0][:, 0:256], in_=wgt[:, 0:256])
         nc.sync.dma_start(out=x[0][:], in_=x_rows[:, 0, :])
-        nc.sync.dma_start(out=wg[0][:], in_=wgt[:, 0:J])
+        nc.sync.dma_start(out=wg[0][:, 256:J], in_=wgt[:, 256:J])
         nc.sync.dma_start(out=wg[1][:], in_=wgt[:, J : 2 * J])
+        nc.sync.dma_start(out=wg[2][:], in_=wgt[:, 2 * J : 3 * J])
         nc.sync.dma_start(out=x[1][:], in_=x_rows[:, 1, :])
         nc.sync.dma_start(out=w4_raw[:].bitcast(I32), in_=w4_words[0].bitcast(I32))
-        nc.sync.dma_start(out=wg[2][:], in_=wgt[:, 2 * J : 3 * J])
-        nc.scalar.dma_start(out=bias[:], in_=b.rearrange("(p t) -> p t", t=PACK))
+        nc.sync.dma_start(out=bias[:], in_=b.rearrange("(p t) -> p t", t=PACK))
         nc.sync.dma_start(out=x[2][:], in_=x_rows[:, 2, :])
         nc.sync.dma_start(out=wd_raw[:], in_=wd.rearrange("(p i) n -> p i n", i=PACK))
         nc.sync.dma_start(out=x[3][:], in_=x_rows[:, 3, :])
@@ -77,16 +80,16 @@ def tile_list_dl_relus_biasP_kernel(
         y_rows = out_0.rearrange("(p t) j -> p t j", t=PACK)
         y_words = out_1[0].rearrange("p j i -> p (j i)").bitcast(I32)
         y_s = tile([P, J], U8, "y_s")
-        SUB = {4: 0}
-        AFTER = {2: "xb1"}
+        SUB = {3: 0, 4: 1}
+        AFTER = {}
         for u, (c, j0, w) in enumerate(units):
             if u in SUB:
-                both = tile([P, 3 * 256], F32, "both%d" % u)
+                both = tile([P, w + 512], F32, "both%d" % u)
                 high[u] = both[:, 0 : 2 * w].rearrange("p (i j) -> p i j", i=2)
-                xb[SUB[u]] = both[:, 256:768].bitcast(BF16).rearrange("p (j i) -> p j i", i=PACK)
-        last = tile([P, PACK * 256], F32, "last")
-        xb[3] = last[:, 512:1024].bitcast(BF16).rearrange("p (j i) -> p j i", i=PACK)
-        last4 = last[:].rearrange("p (i j) -> p i j", i=PACK)
+                xb[SUB[u]] = both[:, w : w + 512].bitcast(BF16).rearrange("p (j i) -> p j i", i=PACK)
+        last = tile([P, 5 * 256], F32, "last")
+        xb[2] = last[:, 768:1280].bitcast(BF16).rearrange("p (j i) -> p j i", i=PACK)
+        last4 = last[:, 0:1024].rearrange("p (i j) -> p i j", i=PACK)
         for u, (c, j0, w) in enumerate(units):
             if u not in xb:
                 xb[u] = tile([P, w, PACK], BF16, "xb%d" % u)[:]
@@ -124,6 +127,9 @@ def tile_list_dl_relus_biasP_kernel(
                 out=xb[u].rearrange("p (g e) i -> p g i e", e=4),
                 in_=last4[:, :, j0 - 256 : j0 - 256 + w].rearrange("p i (g e) -> p g i e", e=4), func=ACT.Copy
             )
+
+        def glp(i, c, j0, w):
+            gather(low[c][:, i, j0 : j0 + w], i, c, j0, w)
 
         def gh(i, u):
             c, j0, w = units[u]
@@ -190,10 +196,11 @@ def tile_list_dl_relus_biasP_kernel(
                             total[:, t, :], bank[:, t - t0, :], 0.0, bias[:, t : t + 1], ALU.max, ALU.add
                         )
                 else:
-                    nc.scalar.activation(out=total[:, t0 : t0 + per_bank, :], in_=bank[:], func=ACT.Relu)
+                    relu = tile([P, per_bank, w], F32, "relu%d_%d" % (u, t0))
+                    nc.scalar.activation(out=relu[:], in_=bank[:], func=ACT.Relu)
                     for t in range(t0, t0 + per_bank):
                         nc.scalar.activation(
-                            out=total[:, t, :], in_=total[:, t, :], func=ACT.Identity, bias=bias[:, t : t + 1]
+                            out=total[:, t, :], in_=relu[:, t - t0, :], func=ACT.Identity, bias=bias[:, t : t + 1]
                         )
 
         def store(u):
@@ -202,7 +209,7 @@ def tile_list_dl_relus_biasP_kernel(
 
         def ybf(u, eng):
             c, j0, w = units[u]
-            y_b[u] = tile([P, w, PACK], BF16, "y_b%d" % u)
+            y_b[u] = tile([P, w, PACK], BF16, "relu3_2" if u == 2 else "y_b%d" % u)
             woven = y_b[u][:].rearrange("p (g e) t -> p g t e", e=4)
             source = totals[u][:].rearrange("p t (g e) -> p g t e", e=4)
             if eng == "S":
@@ -216,9 +223,12 @@ def tile_list_dl_relus_biasP_kernel(
             quantise(y_q[:], y_s[:, j0 : j0 + w], y_b[u][:])
             nc.sync.dma_start(out=y_words[:, j0 : j0 + w], in_=y_q[:].bitcast(I32))
 
-        gl(0,0)
-        gl(0,1)
         s4copy()
+        gather(low[0][:, 0, 0:256], 0, 0, 0, 256)
+        gather(low[0][:, 0, 256:512], 0, 0, 256, 256)
+        gl(0,1)
+        ga(0)
+        g4(0,256,256)
         w4copy()
         gl(1,0)
         weave(0,0)
@@ -226,50 +236,48 @@ def tile_list_dl_relus_biasP_kernel(
         gl(1,1)
         weave(1,0)
         weave(4,0)
-        ga(0)
         ga(1)
         weave(2,0)
-        g4(0,256,256)
         g4(1,256,256)
         wdweave()
         gh(2,0)
         gh(2,1)
+        gh(2,2)
         gh(2,3)
         gh(2,4)
+        g4(2,256,256)
         gh(3,0)
         weave(0,1)
         gh(3,1)
         weave(1,1)
         qwd()
-        gh(3,3)
-        weave(3,1)
-        q(0)
-        mm(0)
-        gh(3,4)
-        weave(4,1)
-        q(1)
-        mm(1)
-        epi(0)
-        gh(2,2)
         gh(3,2)
         weave(2,1)
-        q(3)
-        mm(3)
-        g4(2,256,256)
-        g4(3,256,128)
-        weave4(5)
-        q(4)
-        mm(4)
-        g4(3,384,128)
-        weave4(6)
+        q(0)
+        mm(0)
+        gh(3,3)
+        q(1)
+        mm(1)
+        weave(3,1)
+        gh(3,4)
         q(2)
         mm(2)
+        epi(0)
+        weave(4,1)
+        g4(3,256,128)
+        q(3)
+        mm(3)
+        g4(3,384,128)
         epi(1,0)
-        q(5)
-        q(6)
+        weave4(5)
+        weave4(6)
+        q(4)
+        mm(4)
         epi(2,1)
         store(2)
+        q(5)
         mm(5)
+        q(6)
         epi(3)
         mm(6)
         ybf(2,"S")

@@ -6,6 +6,10 @@ K, N, T, J = 512, 512, 2048, 512
 PICKS = 3
 P = 128
 PACK = 4
+HALF = J // 2
+QUARTER = J // 4
+BANK = 512
+BANKS = 8
 FLOPS = 2 * 2 * K * N * J * PICKS
 
 F32 = mybir.dt.float32
@@ -19,8 +23,13 @@ FP4X4 = mybir.dt.float4_e2m1fn_x4
 ALU = mybir.AluOpType
 ACT = mybir.ActivationFunctionType
 
-UNITS = [(0, 0, 256), (1, 0, 256), (2, 0, 256), (0, 256, 256), (1, 256, 256), (2, 256, 128), (2, 384, 128)]
-VECTOR_SLICES = ((0, 2), (3, 0))
+UNITS = [(c, j0, HALF) for j0 in (0, HALF) for c in range(PICKS)][:-1]
+PAIRED = len(UNITS)
+UNITS = UNITS + [(PICKS - 1, j0, QUARTER) for j0 in (HALF, HALF + QUARTER)]
+LAST = len(UNITS) - 1
+QUANTISE_LAG = 2
+POOL_LAG = 4
+VECTOR_BANK = (0, 2)
 
 
 def tile_list_dl_relus_biasP_kernel(
@@ -34,265 +43,198 @@ def tile_list_dl_relus_biasP_kernel(
         def tile(shape, dtype, name):
             return sb.tile(shape, dtype, name=name, align_bytes=64)
 
+        def as_woven(words):
+            return words.bitcast(BF16).rearrange("p (j i) -> p j i", i=PACK)
+
         lists = sb.tile([P, PICKS * J // 16], U16, name="lists")
-        x = [tile([P, T], F32, "x%d" % i) for i in range(PACK)]
-        wg = [tile([P, J], F32, "wg%d" % c) for c in range(PICKS)]
+        planes = [tile([P, T], F32, "plane%d" % i) for i in range(PACK)]
+        wgt0 = [tile([P, HALF], F32, "wgt0_%d" % h) for h in range(2)]
+        wgt_rest = {c: tile([P, J], F32, "wgt%d" % c) for c in range(1, PICKS)}
         w4_raw = tile([P, 2 * N], U8, "w4_raw")
         s4_raw = tile([P, N], U8, "s4_raw")
         wd_raw = tile([P, PACK, N], F32, "wd_raw")
         bias = tile([P, PACK], F32, "bias")
-        x_rows = xT.rearrange("(p i) t -> p i t", i=PACK)
+
+        def load_plane(i):
+            nc.sync.dma_start(out=planes[i][:], in_=xT.rearrange("(p i) t -> p i t", i=PACK)[:, i, :])
+
         nc.sync.dma_start(lists[:], offs)
-        s4_rows = tile([P, N // 4], I32, "s4_rows")
-        for q in range(4):
-            nc.scalar.dma_start(
-                out=s4_rows[32 * q : 32 * q + 4, :], in_=w4_scales[0, 4 * q : 4 * q + 4, :].bitcast(I32)
-            )
-        nc.vector.memset(s4_raw[:].bitcast(I32), 0)
-        for q in range(4):
-            nc.vector.tensor_copy(out=s4_raw[32 * q : 32 * q + 4, :].bitcast(I32), in_=s4_rows[32 * q : 32 * q + 4, :])
-        nc.sync.dma_start(out=wg[0][:, 0:256], in_=wgt[:, 0:256])
-        nc.sync.dma_start(out=x[0][:], in_=x_rows[:, 0, :])
-        nc.sync.dma_start(out=wg[0][:, 256:J], in_=wgt[:, 256:J])
-        nc.sync.dma_start(out=wg[1][:], in_=wgt[:, J : 2 * J])
-        nc.sync.dma_start(out=wg[2][:], in_=wgt[:, 2 * J : 3 * J])
-        nc.sync.dma_start(out=x[1][:], in_=x_rows[:, 1, :])
+        nc.sync.dma_start(out=wgt0[0][:], in_=wgt[:, 0:HALF])
+        load_plane(0)
+        nc.sync.dma_start(out=wgt0[1][:], in_=wgt[:, HALF:J])
+        for c in range(1, PICKS):
+            nc.sync.dma_start(out=wgt_rest[c][:], in_=wgt[:, c * J : (c + 1) * J])
+        load_plane(1)
         nc.sync.dma_start(out=w4_raw[:].bitcast(I32), in_=w4_words[0].bitcast(I32))
-        nc.sync.dma_start(out=bias[:], in_=b.rearrange("(p t) -> p t", t=PACK))
-        nc.sync.dma_start(out=x[2][:], in_=x_rows[:, 2, :])
+        nc.gpsimd.memset(s4_raw[:].bitcast(I32), 0)
+        for quad in range(4):
+            nc.sync.dma_start(
+                out=s4_raw[32 * quad : 32 * quad + 4, :].bitcast(I32),
+                in_=w4_scales[0, 4 * quad : 4 * quad + 4, :].bitcast(I32),
+            )
+        load_plane(2)
         nc.sync.dma_start(out=wd_raw[:], in_=wd.rearrange("(p i) n -> p i n", i=PACK))
-        nc.sync.dma_start(out=x[3][:], in_=x_rows[:, 3, :])
+        load_plane(3)
+        nc.sync.dma_start(out=bias[:], in_=b.rearrange("(p t) -> p t", t=PACK))
 
-        w4 = tile([P, 2 * N], U8, "w4")
-        s4 = tile([P, N], U8, "s4")
-        units = UNITS
-        low = [tile([P, 2, J], F32, "low%d" % c) for c in range(PICKS)]
-        xq = [tile([P, w], U32, "xq%d" % u) for u, (c, j0, w) in enumerate(units)]
-        xs = [tile([P, w], U8, "xs%d" % u) for u, (c, j0, w) in enumerate(units)]
-        wd_b = tile([P, N, PACK], BF16, "wd_b")
-        wd_q = tile([P, N], U32, "wd_q")
-        wd_s = tile([P, N], U8, "wd_s")
-        xb = {}
-        high = {}
-        totals = {}
-        banks = {}
-        y_b = {}
-        y_rows = out_0.rearrange("(p t) j -> p t j", t=PACK)
-        y_words = out_1[0].rearrange("p j i -> p (j i)").bitcast(I32)
-        y_s = tile([P, J], U8, "y_s")
-        SUB = {3: 0, 4: 1}
-        AFTER = {}
-        for u, (c, j0, w) in enumerate(units):
-            if u in SUB:
-                both = tile([P, w + 512], F32, "both%d" % u)
-                high[u] = both[:, 0 : 2 * w].rearrange("p (i j) -> p i j", i=2)
-                xb[SUB[u]] = both[:, w : w + 512].bitcast(BF16).rearrange("p (j i) -> p j i", i=PACK)
-        last = tile([P, 5 * 256], F32, "last")
-        xb[2] = last[:, 768:1280].bitcast(BF16).rearrange("p (j i) -> p j i", i=PACK)
-        last4 = last[:, 0:1024].rearrange("p (i j) -> p i j", i=PACK)
-        for u, (c, j0, w) in enumerate(units):
-            if u not in xb:
-                xb[u] = tile([P, w, PACK], BF16, "xb%d" % u)[:]
-
-        def s4copy():
-            nc.vector.tensor_copy(
-                out=s4[:].rearrange("p (t q) -> p t q", t=PACK),
-                in_=s4_raw[:].rearrange("p (q t) -> p t q", t=PACK),
-            )
-
-        def w4copy():
-            nc.scalar.copy(
-                out=w4[:].bitcast(U16).rearrange("p (t q) -> p t q", t=PACK),
-                in_=w4_raw[:].bitcast(U16).rearrange("p (q t) -> p t q", t=PACK),
-            )
+        lower = [tile([P, 2, J if c < PICKS - 1 else HALF], F32, "lower%d" % c) for c in range(PICKS)]
+        upper, woven = {}, {}
+        for u in range(PICKS, PAIRED):
+            shared = tile([P, 3 * HALF], F32, "shared%d" % u)
+            upper[u] = shared[:, 0 : 2 * HALF].rearrange("p (i j) -> p i j", i=2)
+            woven[u - PICKS] = as_woven(shared[:, HALF : 3 * HALF])
+        shared = tile([P, PACK * HALF], F32, "shared_four")
+        four = shared[:].rearrange("p (i j) -> p i j", i=PACK)
+        woven[PAIRED - PICKS] = as_woven(shared[:, 2 * HALF : PACK * HALF])
+        for u in range(PICKS):
+            upper[u] = tile([P, 2, HALF], F32, "upper%d" % u)[:]
+        for u in range(PICKS, len(UNITS)):
+            woven[u] = tile([P, UNITS[u][2], PACK], BF16, "woven%d" % u)[:]
+        x_codes = [tile([P, w], U32, "x_codes%d" % u) for u, (c, j0, w) in enumerate(UNITS)]
+        x_scales = [tile([P, w], U8, "x_scales%d" % u) for u, (c, j0, w) in enumerate(UNITS)]
 
         def gather(dst, i, c, j0, w):
             first = (c * J + j0) // 16
-            nc.vector.tensor_tensor(
-                dst, x[i][:].indirect(lists[:, first : first + w // 16]), wg[c][:, j0 : j0 + w], ALU.mult
-            )
+            weights = wgt_rest[c][:, j0 : j0 + w] if c else wgt0[j0 // HALF][:]
+            nc.vector.tensor_tensor(dst, planes[i][:].indirect(lists[:, first : first + w // 16]), weights, ALU.mult)
 
-        def gl(i, c):
-            gather(low[c][:, i, :], i, c, 0, J)
-
-        def ga(i):
-            gather(low[2][:, i, 0:256], i, 2, 0, 256)
-
-        def g4(i, j0, w):
-            gather(last4[:, i, j0 - 256 : j0 - 256 + w], i, 2, j0, w)
-
-        def weave4(u):
-            c, j0, w = units[u]
+        def weave_pair(u, pair, src):
             nc.scalar.activation(
-                out=xb[u].rearrange("p (g e) i -> p g i e", e=4),
-                in_=last4[:, :, j0 - 256 : j0 - 256 + w].rearrange("p i (g e) -> p g i e", e=4), func=ACT.Copy
+                out=woven[u][:, :, 2 * pair : 2 * pair + 2], in_=src.rearrange("p i j -> p j i"), func=ACT.Copy
             )
 
-        def glp(i, c, j0, w):
-            gather(low[c][:, i, j0 : j0 + w], i, c, j0, w)
-
-        def gh(i, u):
-            c, j0, w = units[u]
-            if u not in high:
-                high[u] = tile([P, 2, w], F32, AFTER.get(u, "high%d" % u))[:]
-            gather(high[u][:, i - 2, :], i, c, j0, w)
-
-        def weave(u, half):
-            c, j0, w = units[u]
-            src = low[c][:, :, j0 : j0 + w] if half == 0 else high[u]
-            nc.scalar.activation(
-                out=xb[u][:, :, 2 * half : 2 * half + 2], in_=src.rearrange("p i j -> p j i"), func=ACT.Copy
-            )
+        def four_way(dst, src):
+            return dst.rearrange("p (g e) i -> p g i e", e=4), src.rearrange("p i (g e) -> p g i e", e=4)
 
         def quantise(codes, scales, src):
             nc.vector.quantize_mx(out=codes.bitcast(FP8X4), scales=scales, in_=src.rearrange("p j i -> p (j i)"))
 
-        def q(u):
-            quantise(xq[u][:], xs[u][:], xb[u])
+        w4 = tile([P, 2 * N], U8, "w4")
+        nc.scalar.copy(
+            out=w4[:].bitcast(U16).rearrange("p (t q) -> p t q", t=PACK),
+            in_=w4_raw[:].bitcast(U16).rearrange("p (q t) -> p t q", t=PACK),
+        )
 
-        def wdweave():
-            nc.scalar.activation(
-                out=wd_b[:].rearrange("p (t q) i -> p q i t", t=PACK),
-                in_=wd_raw[:].rearrange("p i (q t) -> p q i t", t=PACK),
-                func=ACT.Copy,
-            )
+        for i in range(2):
+            for c in range(PICKS):
+                ranges = [(0, J)] if c == 1 else [(0, HALF), (HALF, HALF)]
+                for j0, w in ranges:
+                    unpaired = (c, j0) == (PICKS - 1, HALF)
+                    gather(four[:, i, :] if unpaired else lower[c][:, i, j0 : j0 + w], i, c, j0, w)
+                    for u in range(PAIRED):
+                        if i == 1 and UNITS[u][0] == c and j0 <= UNITS[u][1] < j0 + w:
+                            weave_pair(u, 0, lower[c][:, :, UNITS[u][1] : UNITS[u][1] + HALF])
 
-        def qwd():
-            quantise(wd_q[:], wd_s[:], wd_b[:])
+        s4 = tile([P, N], U8, "s4")
+        nc.vector.tensor_copy(
+            out=s4[:].rearrange("p (t q) -> p t q", t=PACK), in_=s4_raw[:].rearrange("p (q t) -> p t q", t=PACK)
+        )
+        wd_woven = tile([P, N, PACK], BF16, "wd_woven")
+        nc.scalar.activation(
+            out=wd_woven[:].rearrange("p (t q) i -> p q i t", t=PACK),
+            in_=wd_raw[:].rearrange("p i (q t) -> p q i t", t=PACK),
+            func=ACT.Copy,
+        )
+        for u in range(PAIRED):
+            gather(upper[u][:, 0, :], 2, *UNITS[u])
 
-        def mm(u):
-            c, j0, w = units[u]
-            per_bank = J // w
-            totals[u] = tile([P, PACK, w], F32, "total%d" % u)
-            for t0 in range(0, PACK, per_bank):
-                bank = ps.tile([P, per_bank, w], F32, name="acc", tag="bank%d" % (len(banks) % 8))
+        def finish_unit(u):
+            c, j0, w = UNITS[u]
+            if u < PAIRED:
+                gather(upper[u][:, 1, :], 3, c, j0, w)
+                weave_pair(u, 1, upper[u])
+                return
+            if u == PAIRED:
+                gather(four[:, 2, :], 2, c, HALF, HALF)
+            cols = slice(j0 - HALF, j0 - HALF + w)
+            gather(four[:, 3, cols], 3, c, j0, w)
+            dst, src = four_way(woven[u], four[:, :, cols])
+            nc.scalar.activation(out=dst, in_=src, func=ACT.Copy)
+
+        banks = {}
+
+        def project(u, wd_codes, wd_scales):
+            w = UNITS[u][2]
+            quantise(x_codes[u][:], x_scales[u][:], woven[u])
+            for t0 in range(0, PACK, BANK // w):
+                bank = ps.tile([P, BANK // w, w], F32, name="acc", tag="bank%d" % (len(banks) % BANKS))
                 banks[u, t0] = bank
-                for t in range(t0, t0 + per_bank):
+                for t in range(t0, t0 + BANK // w):
                     cols = slice(t * P, (t + 1) * P)
                     nc.tensor.matmul_mx(
-                        bank[:, t - t0, :], lhsT=w4[:, 2 * t * P : 2 * (t + 1) * P].bitcast(FP4X4), lhsT_scale=s4[:, cols],
-                        rhs=xq[u][:].bitcast(FP8X4), rhs_scale=xs[u][:], start=True, stop=False,
+                        bank[:, t - t0, :],
+                        lhsT=w4[:, 2 * t * P : 2 * (t + 1) * P].bitcast(FP4X4), lhsT_scale=s4[:, cols],
+                        rhs=x_codes[u][:].bitcast(FP8X4), rhs_scale=x_scales[u][:], start=True, stop=False,
                     )
                     nc.tensor.matmul_mx(
-                        bank[:, t - t0, :], lhsT=wd_q[:, cols].bitcast(FP8X4), lhsT_scale=wd_s[:, cols],
-                        rhs=xq[u][:].bitcast(FP8X4), rhs_scale=xs[u][:], start=False, stop=True,
+                        bank[:, t - t0, :],
+                        lhsT=wd_codes[:, cols].bitcast(FP8X4), lhsT_scale=wd_scales[:, cols],
+                        rhs=x_codes[u][:].bitcast(FP8X4), rhs_scale=x_scales[u][:], start=False, stop=True,
                     )
 
-        def epi(u, before=None):
-            c, j0, w = units[u]
-            per_bank = J // w
-            total = totals[u]
-            for t0 in range(0, PACK, per_bank):
-                bank = banks[u, t0]
+        sums = {}
+
+        def pool(u):
+            c, j0, w = UNITS[u]
+            total = tile([P, PACK, w], F32, "total%d" % u)
+            for t0 in range(0, PACK, BANK // w):
+                bank, slices = banks[u, t0], range(t0, t0 + BANK // w)
                 if c > 0:
-                    off = j0 - units[before][1]
-                    nc.vector.scalar_tensor_tensor(
-                        total[:, t0 : t0 + per_bank, :], bank[:], 0.0,
-                        totals[before][:, t0 : t0 + per_bank, off : off + w], ALU.max, ALU.add
-                    )
-                elif (u, t0) in VECTOR_SLICES:
-                    for t in range(t0, t0 + per_bank):
+                    before = sums[c - 1, j0 // HALF][:, t0 : slices.stop, j0 % HALF : j0 % HALF + w]
+                    nc.vector.scalar_tensor_tensor(total[:, t0 : slices.stop, :], bank[:], 0.0, before, ALU.max, ALU.add)
+                elif (u, t0) == VECTOR_BANK:
+                    for t in slices:
                         nc.vector.tensor_scalar(
                             total[:, t, :], bank[:, t - t0, :], 0.0, bias[:, t : t + 1], ALU.max, ALU.add
                         )
                 else:
-                    relu = tile([P, per_bank, w], F32, "relu%d_%d" % (u, t0))
+                    relu = tile([P, BANK // w, w], F32, "relu%d_%d" % (u, t0))
                     nc.scalar.activation(out=relu[:], in_=bank[:], func=ACT.Relu)
-                    for t in range(t0, t0 + per_bank):
+                    for t in slices:
                         nc.scalar.activation(
                             out=total[:, t, :], in_=relu[:, t - t0, :], func=ACT.Identity, bias=bias[:, t : t + 1]
                         )
+            sums[c, j0 // HALF] = total
+            if c == PICKS - 1:
+                nc.sync.dma_start(out=out_0.rearrange("(p t) j -> p t j", t=PACK)[:, :, j0 : j0 + w], in_=total[:])
+            return total
 
-        def store(u):
-            c, j0, w = units[u]
-            nc.sync.dma_start(out=y_rows[:, :, j0 : j0 + w], in_=totals[u][:])
+        y_codes = [tile([P, HALF], U32, "y_codes%d" % h) for h in range(2)]
+        y_scales = tile([P, J], U8, "y_scales")
+        y_words = out_1[0].rearrange("p j i -> p (j i)").bitcast(I32)
 
-        def ybf(u, eng):
-            c, j0, w = units[u]
-            y_b[u] = tile([P, w, PACK], BF16, "relu3_2" if u == 2 else "y_b%d" % u)
-            woven = y_b[u][:].rearrange("p (g e) t -> p g t e", e=4)
-            source = totals[u][:].rearrange("p t (g e) -> p g t e", e=4)
-            if eng == "S":
-                nc.scalar.activation(out=woven, in_=source, func=ACT.Copy)
+        def hand_on(u, total):
+            c, j0, w = UNITS[u]
+            y_woven = tile([P, w, PACK], BF16, "y_woven%d" % u if j0 else "relu%d_%d" % (PICKS, BANK // w))
+            dst, src = four_way(y_woven[:], total[:])
+            if u < LAST:
+                nc.scalar.activation(out=dst, in_=src, func=ACT.Copy)
             else:
-                nc.vector.tensor_copy(out=woven, in_=source)
+                nc.vector.tensor_copy(out=dst, in_=src)
+            h = j0 // HALF
+            quantise(y_codes[h][:, j0 % HALF : j0 % HALF + w], y_scales[:, j0 : j0 + w], y_woven[:])
+            if (j0 + w) % HALF == 0:
+                nc.sync.dma_start(out=y_words[:, h * HALF : (h + 1) * HALF], in_=y_codes[h][:].bitcast(I32))
 
-        def yq(u):
-            c, j0, w = units[u]
-            y_q = tile([P, w], U32, "y_q%d" % u)
-            quantise(y_q[:], y_s[:, j0 : j0 + w], y_b[u][:])
-            nc.sync.dma_start(out=y_words[:, j0 : j0 + w], in_=y_q[:].bitcast(I32))
+        wd_scales = tile([P, N], U8, "wd_scales")
+        totals = {}
+        for s in range(len(UNITS) + POOL_LAG + 1):
+            if s < len(UNITS):
+                finish_unit(s)
+            if s == QUANTISE_LAG - 1:
+                wd_codes = tile([P, N], U32, "wgt0_0")
+                quantise(wd_codes[:], wd_scales[:], wd_woven[:])
+            if 0 <= s - QUANTISE_LAG <= LAST:
+                project(s - QUANTISE_LAG, wd_codes, wd_scales)
+            if 0 <= s - POOL_LAG <= LAST:
+                totals[s - POOL_LAG] = pool(s - POOL_LAG)
+            done = s - POOL_LAG - 1
+            if done >= 0 and UNITS[done][0] == PICKS - 1:
+                hand_on(done, totals[done])
 
-        s4copy()
-        gather(low[0][:, 0, 0:256], 0, 0, 0, 256)
-        gather(low[0][:, 0, 256:512], 0, 0, 256, 256)
-        gl(0,1)
-        ga(0)
-        g4(0,256,256)
-        w4copy()
-        gl(1,0)
-        weave(0,0)
-        weave(3,0)
-        gl(1,1)
-        weave(1,0)
-        weave(4,0)
-        ga(1)
-        weave(2,0)
-        g4(1,256,256)
-        wdweave()
-        gh(2,0)
-        gh(2,1)
-        gh(2,2)
-        gh(2,3)
-        gh(2,4)
-        g4(2,256,256)
-        gh(3,0)
-        weave(0,1)
-        gh(3,1)
-        weave(1,1)
-        qwd()
-        gh(3,2)
-        weave(2,1)
-        q(0)
-        mm(0)
-        gh(3,3)
-        q(1)
-        mm(1)
-        weave(3,1)
-        gh(3,4)
-        q(2)
-        mm(2)
-        epi(0)
-        weave(4,1)
-        g4(3,256,128)
-        q(3)
-        mm(3)
-        g4(3,384,128)
-        epi(1,0)
-        weave4(5)
-        weave4(6)
-        q(4)
-        mm(4)
-        epi(2,1)
-        store(2)
-        q(5)
-        mm(5)
-        q(6)
-        epi(3)
-        mm(6)
-        ybf(2,"S")
-        epi(4,3)
-        yq(2)
-        epi(5,4)
-        store(5)
-        ybf(5,"S")
-        epi(6,4)
-        store(6)
-        yq(5)
-        ybf(6,"V")
-        yq(6)
-        for k in range(4):
-            queue = nc.scalar if k % 2 else nc.sync
+        for quad in range(4):
+            queue = nc.scalar if quad % 2 else nc.sync
             queue.dma_start(
-                out=out_2[0, 4 * k : 4 * k + 4, :].bitcast(I32), in_=y_s[32 * k : 32 * k + 4, :].bitcast(I32)
+                out=out_2[0, 4 * quad : 4 * quad + 4, :].bitcast(I32),
+                in_=y_scales[32 * quad : 32 * quad + 4, :].bitcast(I32),
             )

from contextlib import ExitStack

import concourse.mybir as mybir

K, N, T, J = 512, 512, 2048, 512
PICKS = 3
P = 128
PACK = 4
HALF = J // 2
QUARTER = J // 4
BANK = 512
BANKS = 8
FLOPS = 2 * 2 * K * N * J * PICKS

F32 = mybir.dt.float32
BF16 = mybir.dt.bfloat16
I32 = mybir.dt.int32
U32 = mybir.dt.uint32
U16 = mybir.dt.uint16
U8 = mybir.dt.uint8
FP8X4 = mybir.dt.float8_e4m3fn_x4
FP4X4 = mybir.dt.float4_e2m1fn_x4
ALU = mybir.AluOpType
ACT = mybir.ActivationFunctionType

UNITS = [(c, j0, HALF) for j0 in (0, HALF) for c in range(PICKS)][:-1]
PAIRED = len(UNITS)
UNITS = UNITS + [(PICKS - 1, j0, QUARTER) for j0 in (HALF, HALF + QUARTER)]
LAST = len(UNITS) - 1
QUANTISE_LAG = 2
POOL_LAG = 4
VECTOR_BANK = (0, 2)


def tile_list_dl_relus_biasP_kernel(
    tc, xT, wgt, w4_words, w4_scales, wd, b, offs, out_0, out_1, out_2
):
    nc = tc.nc
    with ExitStack() as ctx:
        sb = ctx.enter_context(tc.tile_pool(name="sb", bufs=1))
        ps = ctx.enter_context(tc.psum_pool(name="ps", bufs=1))

        def tile(shape, dtype, name):
            return sb.tile(shape, dtype, name=name, align_bytes=64)

        def as_woven(words):
            return words.bitcast(BF16).rearrange("p (j i) -> p j i", i=PACK)

        lists = sb.tile([P, PICKS * J // 16], U16, name="lists")
        planes = [tile([P, T], F32, "plane%d" % i) for i in range(PACK)]
        wgt0 = [tile([P, HALF], F32, "wgt0_%d" % h) for h in range(2)]
        wgt_rest = {c: tile([P, J], F32, "wgt%d" % c) for c in range(1, PICKS)}
        w4_raw = tile([P, 2 * N], U8, "w4_raw")
        s4_raw = tile([P, N], U8, "s4_raw")
        wd_raw = tile([P, PACK, N], F32, "wd_raw")
        bias = tile([P, PACK], F32, "bias")

        def load_plane(i):
            nc.sync.dma_start(out=planes[i][:], in_=xT.rearrange("(p i) t -> p i t", i=PACK)[:, i, :])

        nc.sync.dma_start(lists[:], offs)
        nc.sync.dma_start(out=wgt0[0][:], in_=wgt[:, 0:HALF])
        load_plane(0)
        nc.sync.dma_start(out=wgt0[1][:], in_=wgt[:, HALF:J])
        for c in range(1, PICKS):
            nc.sync.dma_start(out=wgt_rest[c][:], in_=wgt[:, c * J : (c + 1) * J])
        load_plane(1)
        nc.sync.dma_start(out=w4_raw[:].bitcast(I32), in_=w4_words[0].bitcast(I32))
        nc.gpsimd.memset(s4_raw[:].bitcast(I32), 0)
        for quad in range(4):
            nc.sync.dma_start(
                out=s4_raw[32 * quad : 32 * quad + 4, :].bitcast(I32),
                in_=w4_scales[0, 4 * quad : 4 * quad + 4, :].bitcast(I32),
            )
        load_plane(2)
        nc.sync.dma_start(out=wd_raw[:], in_=wd.rearrange("(p i) n -> p i n", i=PACK))
        load_plane(3)
        nc.sync.dma_start(out=bias[:], in_=b.rearrange("(p t) -> p t", t=PACK))

        lower = [tile([P, 2, J if c < PICKS - 1 else HALF], F32, "lower%d" % c) for c in range(PICKS)]
        upper, woven = {}, {}
        for u in range(PICKS, PAIRED):
            shared = tile([P, 3 * HALF], F32, "shared%d" % u)
            upper[u] = shared[:, 0 : 2 * HALF].rearrange("p (i j) -> p i j", i=2)
            woven[u - PICKS] = as_woven(shared[:, HALF : 3 * HALF])
        shared = tile([P, PACK * HALF], F32, "shared_four")
        four = shared[:].rearrange("p (i j) -> p i j", i=PACK)
        woven[PAIRED - PICKS] = as_woven(shared[:, 2 * HALF : PACK * HALF])
        for u in range(PICKS):
            upper[u] = tile([P, 2, HALF], F32, "upper%d" % u)[:]
        for u in range(PICKS, len(UNITS)):
            woven[u] = tile([P, UNITS[u][2], PACK], BF16, "woven%d" % u)[:]
        x_codes = [tile([P, w], U32, "x_codes%d" % u) for u, (c, j0, w) in enumerate(UNITS)]
        x_scales = [tile([P, w], U8, "x_scales%d" % u) for u, (c, j0, w) in enumerate(UNITS)]

        def gather(dst, i, c, j0, w):
            first = (c * J + j0) // 16
            weights = wgt_rest[c][:, j0 : j0 + w] if c else wgt0[j0 // HALF][:]
            nc.vector.tensor_tensor(dst, planes[i][:].indirect(lists[:, first : first + w // 16]), weights, ALU.mult)

        def weave_pair(u, pair, src):
            nc.scalar.activation(
                out=woven[u][:, :, 2 * pair : 2 * pair + 2], in_=src.rearrange("p i j -> p j i"), func=ACT.Copy
            )

        def four_way(dst, src):
            return dst.rearrange("p (g e) i -> p g i e", e=4), src.rearrange("p i (g e) -> p g i e", e=4)

        def quantise(codes, scales, src):
            nc.vector.quantize_mx(out=codes.bitcast(FP8X4), scales=scales, in_=src.rearrange("p j i -> p (j i)"))

        w4 = tile([P, 2 * N], U8, "w4")
        nc.scalar.copy(
            out=w4[:].bitcast(U16).rearrange("p (t q) -> p t q", t=PACK),
            in_=w4_raw[:].bitcast(U16).rearrange("p (q t) -> p t q", t=PACK),
        )

        for i in range(2):
            for c in range(PICKS):
                ranges = [(0, J)] if c == 1 else [(0, HALF), (HALF, HALF)]
                for j0, w in ranges:
                    unpaired = (c, j0) == (PICKS - 1, HALF)
                    gather(four[:, i, :] if unpaired else lower[c][:, i, j0 : j0 + w], i, c, j0, w)
                    for u in range(PAIRED):
                        if i == 1 and UNITS[u][0] == c and j0 <= UNITS[u][1] < j0 + w:
                            weave_pair(u, 0, lower[c][:, :, UNITS[u][1] : UNITS[u][1] + HALF])

        s4 = tile([P, N], U8, "s4")
        nc.vector.tensor_copy(
            out=s4[:].rearrange("p (t q) -> p t q", t=PACK), in_=s4_raw[:].rearrange("p (q t) -> p t q", t=PACK)
        )
        wd_woven = tile([P, N, PACK], BF16, "wd_woven")
        nc.scalar.activation(
            out=wd_woven[:].rearrange("p (t q) i -> p q i t", t=PACK),
            in_=wd_raw[:].rearrange("p i (q t) -> p q i t", t=PACK),
            func=ACT.Copy,
        )
        for u in range(PAIRED):
            gather(upper[u][:, 0, :], 2, *UNITS[u])

        def finish_unit(u):
            c, j0, w = UNITS[u]
            if u < PAIRED:
                gather(upper[u][:, 1, :], 3, c, j0, w)
                weave_pair(u, 1, upper[u])
                return
            if u == PAIRED:
                gather(four[:, 2, :], 2, c, HALF, HALF)
            cols = slice(j0 - HALF, j0 - HALF + w)
            gather(four[:, 3, cols], 3, c, j0, w)
            dst, src = four_way(woven[u], four[:, :, cols])
            nc.scalar.activation(out=dst, in_=src, func=ACT.Copy)

        banks = {}

        def project(u, wd_codes, wd_scales):
            w = UNITS[u][2]
            quantise(x_codes[u][:], x_scales[u][:], woven[u])
            for t0 in range(0, PACK, BANK // w):
                bank = ps.tile([P, BANK // w, w], F32, name="acc", tag="bank%d" % (len(banks) % BANKS))
                banks[u, t0] = bank
                for t in range(t0, t0 + BANK // w):
                    cols = slice(t * P, (t + 1) * P)
                    nc.tensor.matmul_mx(
                        bank[:, t - t0, :],
                        lhsT=w4[:, 2 * t * P : 2 * (t + 1) * P].bitcast(FP4X4), lhsT_scale=s4[:, cols],
                        rhs=x_codes[u][:].bitcast(FP8X4), rhs_scale=x_scales[u][:], start=True, stop=False,
                    )
                    nc.tensor.matmul_mx(
                        bank[:, t - t0, :],
                        lhsT=wd_codes[:, cols].bitcast(FP8X4), lhsT_scale=wd_scales[:, cols],
                        rhs=x_codes[u][:].bitcast(FP8X4), rhs_scale=x_scales[u][:], start=False, stop=True,
                    )

        sums = {}

        def pool(u):
            c, j0, w = UNITS[u]
            total = tile([P, PACK, w], F32, "total%d" % u)
            for t0 in range(0, PACK, BANK // w):
                bank, slices = banks[u, t0], range(t0, t0 + BANK // w)
                if c > 0:
                    before = sums[c - 1, j0 // HALF][:, t0 : slices.stop, j0 % HALF : j0 % HALF + w]
                    nc.vector.scalar_tensor_tensor(total[:, t0 : slices.stop, :], bank[:], 0.0, before, ALU.max, ALU.add)
                elif (u, t0) == VECTOR_BANK:
                    for t in slices:
                        nc.vector.tensor_scalar(
                            total[:, t, :], bank[:, t - t0, :], 0.0, bias[:, t : t + 1], ALU.max, ALU.add
                        )
                else:
                    relu = tile([P, BANK // w, w], F32, "relu%d_%d" % (u, t0))
                    nc.scalar.activation(out=relu[:], in_=bank[:], func=ACT.Relu)
                    for t in slices:
                        nc.scalar.activation(
                            out=total[:, t, :], in_=relu[:, t - t0, :], func=ACT.Identity, bias=bias[:, t : t + 1]
                        )
            sums[c, j0 // HALF] = total
            if c == PICKS - 1:
                nc.sync.dma_start(out=out_0.rearrange("(p t) j -> p t j", t=PACK)[:, :, j0 : j0 + w], in_=total[:])
            return total

        y_codes = [tile([P, HALF], U32, "y_codes%d" % h) for h in range(2)]
        y_scales = tile([P, J], U8, "y_scales")
        y_words = out_1[0].rearrange("p j i -> p (j i)").bitcast(I32)

        def hand_on(u, total):
            c, j0, w = UNITS[u]
            y_woven = tile([P, w, PACK], BF16, "y_woven%d" % u if j0 else "relu%d_%d" % (PICKS, BANK // w))
            dst, src = four_way(y_woven[:], total[:])
            if u < LAST:
                nc.scalar.activation(out=dst, in_=src, func=ACT.Copy)
            else:
                nc.vector.tensor_copy(out=dst, in_=src)
            h = j0 // HALF
            quantise(y_codes[h][:, j0 % HALF : j0 % HALF + w], y_scales[:, j0 : j0 + w], y_woven[:])
            if (j0 + w) % HALF == 0:
                nc.sync.dma_start(out=y_words[:, h * HALF : (h + 1) * HALF], in_=y_codes[h][:].bitcast(I32))

        wd_scales = tile([P, N], U8, "wd_scales")
        totals = {}
        for s in range(len(UNITS) + POOL_LAG + 1):
            if s < len(UNITS):
                finish_unit(s)
            if s == QUANTISE_LAG - 1:
                wd_codes = tile([P, N], U32, "wgt0_0")
                quantise(wd_codes[:], wd_scales[:], wd_woven[:])
            if 0 <= s - QUANTISE_LAG <= LAST:
                project(s - QUANTISE_LAG, wd_codes, wd_scales)
            if 0 <= s - POOL_LAG <= LAST:
                totals[s - POOL_LAG] = pool(s - POOL_LAG)
            done = s - POOL_LAG - 1
            if done >= 0 and UNITS[done][0] == PICKS - 1:
                hand_on(done, totals[done])

        for quad in range(4):
            queue = nc.scalar if quad % 2 else nc.sync
            queue.dma_start(
                out=out_2[0, 4 * quad : 4 * quad + 4, :].bitcast(I32),
                in_=y_scales[32 * quad : 32 * quad + 4, :].bitcast(I32),
            )
